import numpy as np
import ml_dtypes


def mxq(x, axis, fmt="e4m3"):
    dtype, down = {"e4m3": (ml_dtypes.float8_e4m3fn, 7), "e5m2": (ml_dtypes.float8_e5m2, 14)}[fmt]
    v = np.moveaxis(np.asarray(x, np.float32).astype(ml_dtypes.bfloat16).astype(np.float64), axis, -1)
    blocks = v.reshape(v.shape[:-1] + (-1, 32))
    amax = np.abs(blocks).max(-1, keepdims=True)
    byte = np.maximum(np.where(amax > 0, np.frexp(amax)[1] - 1 + 127, 0) - down, 1)
    scale = np.exp2(byte - 127.0)
    codes = (blocks / scale).astype(np.float32).astype(dtype).astype(np.float64)
    return np.moveaxis((codes * scale).reshape(v.shape), -1, axis)


WIDE = False


def mx_kscale(k):
    if not WIDE:
        return np.ones(k)
    levels = np.array([10, -10, 5, -5, 0])
    if k % 512:
        return np.exp2(np.random.permutation(np.resize(levels, k // 32))).repeat(32)
    a = np.empty((k // 512, 16))
    for p in range(k // 512):
        a[p, :8] = np.random.permutation(np.resize(levels, 8))
        for g in range(8):
            far = levels[np.abs(levels - a[p, g]) >= 10]
            a[p, g + 8] = far[np.random.randint(len(far))]
    return np.exp2(a.ravel()).repeat(32)


def f64(x):
    return np.asarray(x).astype(np.float64)


def striped(idx):
    return np.tile(idx.reshape(-1, 16).T, (8, 1)).astype(np.uint16)


def unstriped(offs):
    return offs[:16].T.reshape(-1).astype(np.int64)


def pack_weight(w):
    k, n = w.shape
    w = f64(np.asarray(w, np.float32).astype(ml_dtypes.bfloat16)).reshape(k // 32, 32, n)
    amax = np.abs(w).max(1)
    byte = np.clip(np.where(amax > 0, np.frexp(amax)[1] - 1 + 127 - 7, 1), 1, 254)
    scaled = (w * np.exp2(127.0 - byte)[:, None, :]).reshape(k, n).astype(np.float32)
    words = np.ascontiguousarray(scaled.reshape(k // 512, 128, 4, n).transpose(0, 1, 3, 2)).astype(ml_dtypes.float8_e4m3fn).view(np.uint8)
    return words, np.ascontiguousarray(byte.astype(np.uint8).reshape(k // 512, 16, n))


def unpack_weight(words, scales):
    g, p, n, _ = words.shape
    vals = np.ascontiguousarray(words).view(ml_dtypes.float8_e4m3fn).astype(np.float64) * np.repeat(np.exp2(scales.astype(np.float64) - 127.0), 8, axis=1)[..., None]
    return vals.transpose(0, 1, 3, 2).reshape(g * 512, n)


def planes(y):
    n, m = y.shape
    v = y.astype(np.float32).astype(ml_dtypes.bfloat16).astype(np.float64).reshape(n // 32, 32, m)
    top = np.abs(v).max(1)
    byte = np.clip(np.where(top > 0, np.frexp(top)[1] - 1 + 127 - 7, 1), 1, 254)
    codes = (v * np.exp2(127.0 - byte)[:, None, :]).reshape(n, m).astype(np.float32).astype(ml_dtypes.float8_e4m3fn).view(np.uint8)
    words = codes.reshape(n // 512, 128, 4, m).transpose(0, 1, 3, 2)
    return np.ascontiguousarray(words), np.ascontiguousarray(byte.astype(np.uint8).reshape(n // 512, 16, m))


K, T, S, H, N, U = 1024, 1024, 512, 512, 512, 1024


def setup_inputs():
    n = np.random.standard_normal
    s = mx_kscale(K)[:, None]
    u = mx_kscale(H)
    packed_xT = pack_weight(n((K, T)) * s)
    return {
        "x_words": packed_xT[0],
        "x_scales": packed_xT[1],
        "mem": (n((H, U)) * u[:, None]).astype(np.float32),
        "w1": (n((K, N)) / np.sqrt(2 * K) / s).astype(np.float32),
        "ar": (n((H, N)) / np.sqrt(2 * H) / u[:, None]).astype(np.float32),
        "offs": striped(np.random.permutation(T)[:S]),
        "slot": striped(np.random.permutation(U)[:S]),
    }


def reference(x_words, x_scales, mem, w1, ar, offs, slot):
    h = f64(mem)[:, unstriped(slot)]
    xq = unpack_weight(x_words, x_scales)[:, unstriped(offs)]
    out_0 = mxq(f64(ar), 0, "e4m3").T @ mxq(h, 0, "e4m3") + mxq(f64(w1), 0, "e4m3").T @ xq
    return (out_0,) + planes(out_0)

@@ -1,0 +1,174 @@
+from contextlib import ExitStack
+
+import concourse.mybir as mybir
+
+F32 = mybir.dt.float32
+BF16 = mybir.dt.bfloat16
+I32 = mybir.dt.int32
+U32 = mybir.dt.uint32
+U16 = mybir.dt.uint16
+U8 = mybir.dt.uint8
+FP8X4 = mybir.dt.float8_e4m3fn_x4
+
+P = 128
+PACK = 4
+K_PASS = P * PACK
+TABLE = 1024
+PICKED = 512
+CELLS = 512
+HALF = 256
+FLOPS = 2 * 1536 * CELLS * PICKED
+
+
+def tile_picked_ylmu_lin_po_kernel(
+    tc, x_words, x_scales, mem, w1, ar, offs, slot, out_0, out_1, out_2
+):
+    nc = tc.nc
+    with ExitStack() as ctx:
+        sb = ctx.enter_context(tc.tile_pool(name="sb", bufs=1))
+        psum = ctx.enter_context(tc.psum_pool(name="psum", bufs=1))
+
+        offs_sb = sb.tile([P, PICKED // 16], U16, name="offs_sb")
+        slot_sb = sb.tile([P, PICKED // 16], U16, name="slot_sb")
+        nc.sync.dma_start(slot_sb[:], slot)
+        nc.sync.dma_start(offs_sb[:], offs)
+
+        xs_table = sb.tile([P, TABLE], U8, name="xs_table", align_bytes=64)
+        nc.gpsimd.memset(xs_table[:].bitcast(I32), 0)
+        for q in range(4):
+            nc.gpsimd.dma_start(
+                xs_table[32 * q : 32 * q + 8, :].bitcast(I32),
+                x_scales[:, 4 * q : 4 * q + 4, :].bitcast(I32),
+            )
+
+        weights = [ar, w1[0:K_PASS, :], w1[K_PASS : 2 * K_PASS, :]]
+        mem_rows = mem.rearrange("(p j) c -> p j c", j=PACK)
+        mem_sb = [sb.tile([P, TABLE], F32, name=f"mem_sb{j}") for j in range(PACK)]
+        w_raw = [[sb.tile([P, PACK, HALF], F32, name=f"w_raw{g}_{c}") for c in range(2)] for g in range(3)]
+        xw_table = [sb.tile([P, TABLE], I32, name=f"xw_table{g}", align_bytes=64) for g in range(2)]
+
+        def load_mem(j):
+            nc.sync.dma_start(mem_sb[j][:], mem_rows[:, j, :])
+
+        def load_w(g, c):
+            rows = weights[g].rearrange("(p j) c -> p j c", j=PACK)
+            nc.sync.dma_start(w_raw[g][c][:], rows[:, :, c * HALF : (c + 1) * HALF])
+
+        def load_x(g):
+            nc.sync.dma_start(xw_table[g][:], x_words[g].rearrange("p n t -> p (n t)").bitcast(I32))
+
+        load_mem(0)
+        load_mem(1)
+        load_w(0, 0)
+        load_mem(2)
+        load_mem(3)
+        load_w(0, 1)
+        load_w(1, 0)
+        load_x(0)
+        load_w(1, 1)
+        load_w(2, 0)
+        load_w(2, 1)
+        load_x(1)
+
+        w_bf = [sb.tile([P, PACK, P, PACK], BF16, name=f"w_bf{g}", align_bytes=64) for g in range(3)]
+        w_codes = [sb.tile([P, CELLS], U32, name=f"w_codes{g}", align_bytes=64) for g in range(3)]
+        w_scales = [sb.tile([P, CELLS], U8, name=f"w_scales{g}", align_bytes=64) for g in range(3)]
+
+        def deal_w(copy, g, c, lo, hi):
+            src = w_raw[g][c][:].rearrange("p j (m t) -> p m j t", t=PACK)[:, lo:hi]
+            dst = w_bf[g][:].rearrange("p t m j -> p m j t")[:, 64 * c + lo : 64 * c + hi]
+            copy(dst, src)
+
+        def quantize(codes, scales, grouped):
+            nc.vector.quantize_mx(out=codes.bitcast(FP8X4), scales=scales, in_=grouped)
+
+        def quantize_w(g):
+            quantize(w_codes[g][:], w_scales[g][:], w_bf[g][:].rearrange("p t m j -> p (t m j)"))
+
+        h_planes = sb.tile([P, PACK, PICKED], F32, name="h_planes")
+        h_bf = sb.tile([P, PICKED, PACK], BF16, name="h_bf", align_bytes=64)
+        h_codes = sb.tile([P, PICKED], U32, name="h_codes", align_bytes=64)
+        h_scales = sb.tile([P, PICKED], U8, name="h_scales", align_bytes=64)
+        xs = sb.tile([P, PICKED], U8, name="xs", align_bytes=64)
+        xw = [[sb.tile([P, HALF], U32, name=f"xw{g}_{c}", align_bytes=64) for c in range(2)] for g in range(2)]
+
+        def gather_mem(j):
+            nc.vector.tensor_copy(h_planes[:, j, :], mem_sb[j][:].indirect(slot_sb[:]))
+
+        def gather_x(g, c):
+            nc.vector.tensor_copy(
+                xw[g][c][:], xw_table[g][:].bitcast(U32).indirect(offs_sb[:, 16 * c : 16 * (c + 1)])
+            )
+
+        def interleave(copy, dst, src):
+            copy(dst.rearrange("p (c i) t -> p c t i", i=4), src.rearrange("p t (c i) -> p c t i", i=4))
+
+        acc = [[psum.tile([P, HALF], F32, name=f"acc{c}_{t}") for t in range(PACK)] for c in range(2)]
+
+        def product(g, c):
+            cols = slice(c * HALF, (c + 1) * HALF)
+            for t in range(PACK):
+                m = slice(t * P, (t + 1) * P)
+                if g == 0:
+                    rhs, rhs_scale = h_codes[:, cols], h_scales[:, cols]
+                else:
+                    rhs, rhs_scale = xw[g - 1][c][:], xs[4 * (g - 1) : P, cols]
+                nc.tensor.matmul_mx(
+                    out=acc[c][t][:],
+                    lhsT=w_codes[g][:, m].bitcast(FP8X4),
+                    lhsT_scale=w_scales[g][:, m],
+                    rhs=rhs.bitcast(FP8X4),
+                    rhs_scale=rhs_scale,
+                    start=(g == 0),
+                    stop=(g == 2),
+                )
+
+        gather_mem(0)
+        gather_mem(1)
+        deal_w(nc.scalar.copy, 0, 0, 0, 64)
+        nc.vector.tensor_copy(xs[:], xs_table[:].indirect(offs_sb[:]))
+        gather_mem(2)
+        gather_mem(3)
+        deal_w(nc.scalar.copy, 0, 1, 0, 64)
+        interleave(nc.vector.tensor_copy, h_bf[:], h_planes[:])
+        quantize_w(0)
+        quantize(h_codes[:], h_scales[:], h_bf[:].rearrange("p c t -> p (c t)"))
+        deal_w(nc.scalar.copy, 1, 0, 0, 64)
+        product(0, 0)
+        product(0, 1)
+        gather_x(0, 0)
+        gather_x(0, 1)
+        deal_w(nc.scalar.copy, 1, 1, 0, 64)
+        quantize_w(1)
+        product(1, 0)
+        product(1, 1)
+        deal_w(nc.scalar.copy, 2, 0, 0, 64)
+        deal_w(nc.scalar.copy, 2, 1, 0, 24)
+        deal_w(nc.vector.tensor_copy, 2, 1, 24, 64)
+        quantize_w(2)
+
+        y = [sb.tile([P, PACK, HALF], F32, name=f"y{c}") for c in range(2)]
+        y_bf = [sb.tile([P, HALF, PACK], BF16, name=f"y_bf{c}", align_bytes=64) for c in range(2)]
+        y_codes = [sb.tile([P, HALF], U32, name=f"y_codes{c}", align_bytes=64) for c in range(2)]
+        y_scales = sb.tile([P, PICKED], U8, name="y_scales", align_bytes=64)
+        out_rows = out_0.rearrange("(p t) c -> p t c", t=PACK)
+        out_words = out_1[0].rearrange("p c t -> p (c t)").bitcast(I32)
+
+        gather_x(1, 0)
+        gather_x(1, 1)
+        for c in range(2):
+            product(2, c)
+        for c in range(2):
+            cols = slice(c * HALF, (c + 1) * HALF)
+            for t in range(PACK):
+                nc.scalar.copy(y[c][:, t, :], acc[c][t][:])
+            nc.sync.dma_start(out_rows[:, :, cols], y[c][:])
+            interleave(nc.vector.tensor_copy, y_bf[c][:], y[c][:])
+            quantize(y_codes[c][:], y_scales[:, cols], y_bf[c][:].rearrange("p c t -> p (c t)"))
+            nc.sync.dma_start(out_words[:, cols], y_codes[c][:].bitcast(I32))
+        for q in range(4):
+            queue = nc.sync if q % 2 == 0 else nc.scalar
+            queue.dma_start(
+                out_2[0, 4 * q : 4 * q + 4, :].bitcast(I32),
+                y_scales[32 * q : 32 * q + 4, :].bitcast(I32),
+            )

@@ -13,11 +13,16 @@ FP8X4 = mybir.dt.float8_e4m3fn_x4
 P = 128
 PACK = 4
 K_PASS = P * PACK
+QUADRANTS = 4
 TABLE = 1024
 PICKED = 512
 CELLS = 512
-HALF = 256
-FLOPS = 2 * 1536 * CELLS * PICKED
+HALF = PICKED // 2
+LIST_COLUMNS = PICKED // 16
+FLOPS = 2 * 3 * K_PASS * CELLS * PICKED
+
+LAST_WEIGHTS_ON_SCALAR = 44
+LAST_RESULT_ON_SCALAR = 96
 
 
 def tile_picked_ylmu_lin_po_kernel(
@@ -28,145 +33,150 @@ def tile_picked_ylmu_lin_po_kernel(
         sb = ctx.enter_context(tc.tile_pool(name="sb", bufs=1))
         psum = ctx.enter_context(tc.psum_pool(name="psum", bufs=1))
 
-        offs_sb = sb.tile([P, PICKED // 16], U16, name="offs_sb")
-        slot_sb = sb.tile([P, PICKED // 16], U16, name="slot_sb")
-        nc.sync.dma_start(slot_sb[:], slot)
-        nc.sync.dma_start(offs_sb[:], offs)
+        offs_sb = sb.tile([P, LIST_COLUMNS], U16, name="offs_sb")
+        slot_sb = sb.tile([P, LIST_COLUMNS], U16, name="slot_sb")
 
         xs_table = sb.tile([P, TABLE], U8, name="xs_table", align_bytes=64)
-        nc.gpsimd.memset(xs_table[:].bitcast(I32), 0)
-        for q in range(4):
-            nc.gpsimd.dma_start(
-                xs_table[32 * q : 32 * q + 8, :].bitcast(I32),
-                x_scales[:, 4 * q : 4 * q + 4, :].bitcast(I32),
-            )
+        nc.vector.memset(xs_table[:].bitcast(I32), 0)
 
         weights = [ar, w1[0:K_PASS, :], w1[K_PASS : 2 * K_PASS, :]]
+        pieces = [2, 1, 1]
         mem_rows = mem.rearrange("(p j) c -> p j c", j=PACK)
         mem_sb = [sb.tile([P, TABLE], F32, name=f"mem_sb{j}") for j in range(PACK)]
-        w_raw = [[sb.tile([P, PACK, HALF], F32, name=f"w_raw{g}_{c}") for c in range(2)] for g in range(3)]
+        w_raw = [
+            [sb.tile([P, PACK, CELLS // pieces[g]], F32, name=f"w_raw{g}_{piece}") for piece in range(pieces[g])]
+            for g in range(3)
+        ]
         xw_table = [sb.tile([P, TABLE], I32, name=f"xw_table{g}", align_bytes=64) for g in range(2)]
 
         def load_mem(j):
             nc.sync.dma_start(mem_sb[j][:], mem_rows[:, j, :])
 
-        def load_w(g, c):
+        def load_w(g, piece):
             rows = weights[g].rearrange("(p j) c -> p j c", j=PACK)
-            nc.sync.dma_start(w_raw[g][c][:], rows[:, :, c * HALF : (c + 1) * HALF])
+            width = CELLS // pieces[g]
+            nc.sync.dma_start(w_raw[g][piece][:], rows[:, :, piece * width : (piece + 1) * width])
 
         def load_x(g):
             nc.sync.dma_start(xw_table[g][:], x_words[g].rearrange("p n t -> p (n t)").bitcast(I32))
 
         load_mem(0)
+        nc.sync.dma_start(slot_sb[:], slot)
+        for q in range(QUADRANTS):
+            nc.sync.dma_start(
+                xs_table[32 * q : 32 * q + 8, :].bitcast(I32),
+                x_scales[:, 4 * q : 4 * q + 4, :].bitcast(I32),
+            )
         load_mem(1)
         load_w(0, 0)
+        nc.sync.dma_start(offs_sb[:], offs)
         load_mem(2)
         load_mem(3)
         load_w(0, 1)
         load_w(1, 0)
         load_x(0)
-        load_w(1, 1)
         load_w(2, 0)
-        load_w(2, 1)
         load_x(1)
 
         w_bf = [sb.tile([P, PACK, P, PACK], BF16, name=f"w_bf{g}", align_bytes=64) for g in range(3)]
         w_codes = [sb.tile([P, CELLS], U32, name=f"w_codes{g}", align_bytes=64) for g in range(3)]
         w_scales = [sb.tile([P, CELLS], U8, name=f"w_scales{g}", align_bytes=64) for g in range(3)]
 
-        def deal_w(copy, g, c, lo, hi):
-            src = w_raw[g][c][:].rearrange("p j (m t) -> p m j t", t=PACK)[:, lo:hi]
-            dst = w_bf[g][:].rearrange("p t m j -> p m j t")[:, 64 * c + lo : 64 * c + hi]
-            copy(dst, src)
-
         def quantize(codes, scales, grouped):
             nc.vector.quantize_mx(out=codes.bitcast(FP8X4), scales=scales, in_=grouped)
+
+        def deal_views(g, piece):
+            width = P // pieces[g]
+            src = w_raw[g][piece][:].rearrange("p j (m u e) -> p u m j e", u=2, e=2)
+            dst = w_bf[g][:].rearrange("p (u e) m j -> p u m j e", e=2)
+            return dst[:, :, piece * width : (piece + 1) * width], src
 
         def quantize_w(g):
             quantize(w_codes[g][:], w_scales[g][:], w_bf[g][:].rearrange("p t m j -> p (t m j)"))
 
-        h_planes = sb.tile([P, PACK, PICKED], F32, name="h_planes")
+        def regroup(copy, dst, src):
+            copy(dst.rearrange("p (c i) t -> p c t i", i=4), src.rearrange("p t (c i) -> p c t i", i=4))
+
+        h_rows = sb.tile([P, PACK, PICKED], F32, name="h_rows")
         h_bf = sb.tile([P, PICKED, PACK], BF16, name="h_bf", align_bytes=64)
         h_codes = sb.tile([P, PICKED], U32, name="h_codes", align_bytes=64)
         h_scales = sb.tile([P, PICKED], U8, name="h_scales", align_bytes=64)
         xs = sb.tile([P, PICKED], U8, name="xs", align_bytes=64)
-        xw = [[sb.tile([P, HALF], U32, name=f"xw{g}_{c}", align_bytes=64) for c in range(2)] for g in range(2)]
 
-        def gather_mem(j):
-            nc.vector.tensor_copy(h_planes[:, j, :], mem_sb[j][:].indirect(slot_sb[:]))
+        acc = [[psum.tile([P, HALF], F32, name=f"acc{half}_{t}") for t in range(PACK)] for half in range(2)]
 
-        def gather_x(g, c):
-            nc.vector.tensor_copy(
-                xw[g][c][:], xw_table[g][:].bitcast(U32).indirect(offs_sb[:, 16 * c : 16 * (c + 1)])
-            )
+        def columns(half):
+            return slice(half * HALF, (half + 1) * HALF)
 
-        def interleave(copy, dst, src):
-            copy(dst.rearrange("p (c i) t -> p c t i", i=4), src.rearrange("p t (c i) -> p c t i", i=4))
-
-        acc = [[psum.tile([P, HALF], F32, name=f"acc{c}_{t}") for t in range(PACK)] for c in range(2)]
-
-        def product(g, c):
-            cols = slice(c * HALF, (c + 1) * HALF)
+        def product(g, half, codes, scales):
             for t in range(PACK):
-                m = slice(t * P, (t + 1) * P)
-                if g == 0:
-                    rhs, rhs_scale = h_codes[:, cols], h_scales[:, cols]
-                else:
-                    rhs, rhs_scale = xw[g - 1][c][:], xs[4 * (g - 1) : P, cols]
+                dealt = slice(t * P, (t + 1) * P)
                 nc.tensor.matmul_mx(
-                    out=acc[c][t][:],
-                    lhsT=w_codes[g][:, m].bitcast(FP8X4),
-                    lhsT_scale=w_scales[g][:, m],
-                    rhs=rhs.bitcast(FP8X4),
-                    rhs_scale=rhs_scale,
+                    out=acc[half][t][:],
+                    lhsT=w_codes[g][:, dealt].bitcast(FP8X4),
+                    lhsT_scale=w_scales[g][:, dealt],
+                    rhs=codes.bitcast(FP8X4),
+                    rhs_scale=scales,
                     start=(g == 0),
                     stop=(g == 2),
                 )
 
-        gather_mem(0)
-        gather_mem(1)
-        deal_w(nc.scalar.copy, 0, 0, 0, 64)
         nc.vector.tensor_copy(xs[:], xs_table[:].indirect(offs_sb[:]))
-        gather_mem(2)
-        gather_mem(3)
-        deal_w(nc.scalar.copy, 0, 1, 0, 64)
-        interleave(nc.vector.tensor_copy, h_bf[:], h_planes[:])
-        quantize_w(0)
+        for j in range(PACK):
+            nc.vector.tensor_copy(h_rows[:, j, :], mem_sb[j][:].indirect(slot_sb[:]))
+        regroup(nc.vector.tensor_copy, h_bf[:], h_rows[:])
         quantize(h_codes[:], h_scales[:], h_bf[:].rearrange("p c t -> p (c t)"))
-        deal_w(nc.scalar.copy, 1, 0, 0, 64)
-        product(0, 0)
-        product(0, 1)
-        gather_x(0, 0)
-        gather_x(0, 1)
-        deal_w(nc.scalar.copy, 1, 1, 0, 64)
+        for piece in range(pieces[0]):
+            nc.scalar.copy(*deal_views(0, piece))
+        quantize_w(0)
+        for half in range(2):
+            product(0, half, h_codes[:, columns(half)], h_scales[:, columns(half)])
+
+        xw_first = sb.tile([P, PICKED], U32, name="xw_first", align_bytes=64)
+        nc.vector.tensor_copy(xw_first[:], xw_table[0][:].bitcast(U32).indirect(offs_sb[:]))
+        nc.scalar.copy(*deal_views(1, 0))
         quantize_w(1)
-        product(1, 0)
-        product(1, 1)
-        deal_w(nc.scalar.copy, 2, 0, 0, 64)
-        deal_w(nc.scalar.copy, 2, 1, 0, 24)
-        deal_w(nc.vector.tensor_copy, 2, 1, 24, 64)
+        for half in range(2):
+            product(1, half, xw_first[:, columns(half)], xs[:, columns(half)])
+
+        dst, src = deal_views(2, 0)
+        nc.scalar.copy(dst[:, :, :LAST_WEIGHTS_ON_SCALAR], src[:, :, :LAST_WEIGHTS_ON_SCALAR])
+        nc.vector.tensor_copy(dst[:, :, LAST_WEIGHTS_ON_SCALAR:], src[:, :, LAST_WEIGHTS_ON_SCALAR:])
         quantize_w(2)
 
-        y = [sb.tile([P, PACK, HALF], F32, name=f"y{c}") for c in range(2)]
-        y_bf = [sb.tile([P, HALF, PACK], BF16, name=f"y_bf{c}", align_bytes=64) for c in range(2)]
-        y_codes = [sb.tile([P, HALF], U32, name=f"y_codes{c}", align_bytes=64) for c in range(2)]
+        y = [sb.tile([P, PACK, HALF], F32, name=f"y{half}") for half in range(2)]
+        y_bf = [sb.tile([P, HALF, PACK], BF16, name=f"y_bf{half}", align_bytes=64) for half in range(2)]
+        y_codes = [sb.tile([P, HALF], U32, name=f"y_codes{half}", align_bytes=64) for half in range(2)]
         y_scales = sb.tile([P, PICKED], U8, name="y_scales", align_bytes=64)
         out_rows = out_0.rearrange("(p t) c -> p t c", t=PACK)
         out_words = out_1[0].rearrange("p c t -> p (c t)").bitcast(I32)
 
-        gather_x(1, 0)
-        gather_x(1, 1)
-        for c in range(2):
-            product(2, c)
-        for c in range(2):
-            cols = slice(c * HALF, (c + 1) * HALF)
-            for t in range(PACK):
-                nc.scalar.copy(y[c][:, t, :], acc[c][t][:])
-            nc.sync.dma_start(out_rows[:, :, cols], y[c][:])
-            interleave(nc.vector.tensor_copy, y_bf[c][:], y[c][:])
-            quantize(y_codes[c][:], y_scales[:, cols], y_bf[c][:].rearrange("p c t -> p (c t)"))
-            nc.sync.dma_start(out_words[:, cols], y_codes[c][:].bitcast(I32))
-        for q in range(4):
+        for half in range(2):
+            xw_last = sb.tile([P, HALF], U32, name=f"xw_last{half}", align_bytes=64)
+            entries = offs_sb[:, half * LIST_COLUMNS // 2 : (half + 1) * LIST_COLUMNS // 2]
+            nc.vector.tensor_copy(xw_last[:], xw_table[1][:].bitcast(U32).indirect(entries))
+            product(2, half, xw_last[:], xs[4:P, columns(half)])
+
+        def empty_banks(copy, half, first):
+            for t in (first, first + 1):
+                copy(y[half][:, t, :], acc[half][t][:])
+            nc.sync.dma_start(out_rows[:, first : first + 2, columns(half)], y[half][:, first : first + 2, :])
+
+        def hand_on(half):
+            quantize(y_codes[half][:], y_scales[:, columns(half)], y_bf[half][:].rearrange("p c t -> p (c t)"))
+            nc.sync.dma_start(out_words[:, columns(half)], y_codes[half][:].bitcast(I32))
+
+        empty_banks(nc.scalar.copy, 0, 0)
+        empty_banks(nc.vector.tensor_copy, 0, 2)
+        regroup(nc.vector.tensor_copy, y_bf[0][:], y[0][:])
+        hand_on(0)
+        empty_banks(nc.scalar.copy, 1, 0)
+        empty_banks(nc.scalar.copy, 1, 2)
+        regroup(nc.scalar.copy, y_bf[1][:, :LAST_RESULT_ON_SCALAR, :], y[1][:, :, :LAST_RESULT_ON_SCALAR])
+        regroup(nc.vector.tensor_copy, y_bf[1][:, LAST_RESULT_ON_SCALAR:, :], y[1][:, :, LAST_RESULT_ON_SCALAR:])
+        hand_on(1)
+
+        for q in range(QUADRANTS):
             queue = nc.sync if q % 2 == 0 else nc.scalar
             queue.dma_start(
                 out_2[0, 4 * q : 4 * q + 4, :].bitcast(I32),

from contextlib import ExitStack

import concourse.mybir as mybir

F32 = mybir.dt.float32
BF16 = mybir.dt.bfloat16
I32 = mybir.dt.int32
U32 = mybir.dt.uint32
U16 = mybir.dt.uint16
U8 = mybir.dt.uint8
FP8X4 = mybir.dt.float8_e4m3fn_x4

P = 128
PACK = 4
K_PASS = P * PACK
QUADRANTS = 4
TABLE = 1024
PICKED = 512
CELLS = 512
HALF = PICKED // 2
LIST_COLUMNS = PICKED // 16
FLOPS = 2 * 3 * K_PASS * CELLS * PICKED

LAST_WEIGHTS_ON_SCALAR = 44
LAST_RESULT_ON_SCALAR = 96


def tile_picked_ylmu_lin_po_kernel(
    tc, x_words, x_scales, mem, w1, ar, offs, slot, out_0, out_1, out_2
):
    nc = tc.nc
    with ExitStack() as ctx:
        sb = ctx.enter_context(tc.tile_pool(name="sb", bufs=1))
        psum = ctx.enter_context(tc.psum_pool(name="psum", bufs=1))

        offs_sb = sb.tile([P, LIST_COLUMNS], U16, name="offs_sb")
        slot_sb = sb.tile([P, LIST_COLUMNS], U16, name="slot_sb")

        xs_table = sb.tile([P, TABLE], U8, name="xs_table", align_bytes=64)
        nc.vector.memset(xs_table[:].bitcast(I32), 0)

        weights = [ar, w1[0:K_PASS, :], w1[K_PASS : 2 * K_PASS, :]]
        pieces = [2, 1, 1]
        mem_rows = mem.rearrange("(p j) c -> p j c", j=PACK)
        mem_sb = [sb.tile([P, TABLE], F32, name=f"mem_sb{j}") for j in range(PACK)]
        w_raw = [
            [sb.tile([P, PACK, CELLS // pieces[g]], F32, name=f"w_raw{g}_{piece}") for piece in range(pieces[g])]
            for g in range(3)
        ]
        xw_table = [sb.tile([P, TABLE], I32, name=f"xw_table{g}", align_bytes=64) for g in range(2)]

        def load_mem(j):
            nc.sync.dma_start(mem_sb[j][:], mem_rows[:, j, :])

        def load_w(g, piece):
            rows = weights[g].rearrange("(p j) c -> p j c", j=PACK)
            width = CELLS // pieces[g]
            nc.sync.dma_start(w_raw[g][piece][:], rows[:, :, piece * width : (piece + 1) * width])

        def load_x(g):
            nc.sync.dma_start(xw_table[g][:], x_words[g].rearrange("p n t -> p (n t)").bitcast(I32))

        load_mem(0)
        nc.sync.dma_start(slot_sb[:], slot)
        for q in range(QUADRANTS):
            nc.sync.dma_start(
                xs_table[32 * q : 32 * q + 8, :].bitcast(I32),
                x_scales[:, 4 * q : 4 * q + 4, :].bitcast(I32),
            )
        load_mem(1)
        load_w(0, 0)
        nc.sync.dma_start(offs_sb[:], offs)
        load_mem(2)
        load_mem(3)
        load_w(0, 1)
        load_w(1, 0)
        load_x(0)
        load_w(2, 0)
        load_x(1)

        w_bf = [sb.tile([P, PACK, P, PACK], BF16, name=f"w_bf{g}", align_bytes=64) for g in range(3)]
        w_codes = [sb.tile([P, CELLS], U32, name=f"w_codes{g}", align_bytes=64) for g in range(3)]
        w_scales = [sb.tile([P, CELLS], U8, name=f"w_scales{g}", align_bytes=64) for g in range(3)]

        def quantize(codes, scales, grouped):
            nc.vector.quantize_mx(out=codes.bitcast(FP8X4), scales=scales, in_=grouped)

        def deal_views(g, piece):
            width = P // pieces[g]
            src = w_raw[g][piece][:].rearrange("p j (m u e) -> p u m j e", u=2, e=2)
            dst = w_bf[g][:].rearrange("p (u e) m j -> p u m j e", e=2)
            return dst[:, :, piece * width : (piece + 1) * width], src

        def quantize_w(g):
            quantize(w_codes[g][:], w_scales[g][:], w_bf[g][:].rearrange("p t m j -> p (t m j)"))

        def regroup(copy, dst, src):
            copy(dst.rearrange("p (c i) t -> p c t i", i=4), src.rearrange("p t (c i) -> p c t i", i=4))

        h_rows = sb.tile([P, PACK, PICKED], F32, name="h_rows")
        h_bf = sb.tile([P, PICKED, PACK], BF16, name="h_bf", align_bytes=64)
        h_codes = sb.tile([P, PICKED], U32, name="h_codes", align_bytes=64)
        h_scales = sb.tile([P, PICKED], U8, name="h_scales", align_bytes=64)
        xs = sb.tile([P, PICKED], U8, name="xs", align_bytes=64)

        acc = [[psum.tile([P, HALF], F32, name=f"acc{half}_{t}") for t in range(PACK)] for half in range(2)]

        def columns(half):
            return slice(half * HALF, (half + 1) * HALF)

        def product(g, half, codes, scales):
            for t in range(PACK):
                dealt = slice(t * P, (t + 1) * P)
                nc.tensor.matmul_mx(
                    out=acc[half][t][:],
                    lhsT=w_codes[g][:, dealt].bitcast(FP8X4),
                    lhsT_scale=w_scales[g][:, dealt],
                    rhs=codes.bitcast(FP8X4),
                    rhs_scale=scales,
                    start=(g == 0),
                    stop=(g == 2),
                )

        nc.vector.tensor_copy(xs[:], xs_table[:].indirect(offs_sb[:]))
        for j in range(PACK):
            nc.vector.tensor_copy(h_rows[:, j, :], mem_sb[j][:].indirect(slot_sb[:]))
        regroup(nc.vector.tensor_copy, h_bf[:], h_rows[:])
        quantize(h_codes[:], h_scales[:], h_bf[:].rearrange("p c t -> p (c t)"))
        for piece in range(pieces[0]):
            nc.scalar.copy(*deal_views(0, piece))
        quantize_w(0)
        for half in range(2):
            product(0, half, h_codes[:, columns(half)], h_scales[:, columns(half)])

        xw_first = sb.tile([P, PICKED], U32, name="xw_first", align_bytes=64)
        nc.vector.tensor_copy(xw_first[:], xw_table[0][:].bitcast(U32).indirect(offs_sb[:]))
        nc.scalar.copy(*deal_views(1, 0))
        quantize_w(1)
        for half in range(2):
            product(1, half, xw_first[:, columns(half)], xs[:, columns(half)])

        dst, src = deal_views(2, 0)
        nc.scalar.copy(dst[:, :, :LAST_WEIGHTS_ON_SCALAR], src[:, :, :LAST_WEIGHTS_ON_SCALAR])
        nc.vector.tensor_copy(dst[:, :, LAST_WEIGHTS_ON_SCALAR:], src[:, :, LAST_WEIGHTS_ON_SCALAR:])
        quantize_w(2)

        y = [sb.tile([P, PACK, HALF], F32, name=f"y{half}") for half in range(2)]
        y_bf = [sb.tile([P, HALF, PACK], BF16, name=f"y_bf{half}", align_bytes=64) for half in range(2)]
        y_codes = [sb.tile([P, HALF], U32, name=f"y_codes{half}", align_bytes=64) for half in range(2)]
        y_scales = sb.tile([P, PICKED], U8, name="y_scales", align_bytes=64)
        out_rows = out_0.rearrange("(p t) c -> p t c", t=PACK)
        out_words = out_1[0].rearrange("p c t -> p (c t)").bitcast(I32)

        for half in range(2):
            xw_last = sb.tile([P, HALF], U32, name=f"xw_last{half}", align_bytes=64)
            entries = offs_sb[:, half * LIST_COLUMNS // 2 : (half + 1) * LIST_COLUMNS // 2]
            nc.vector.tensor_copy(xw_last[:], xw_table[1][:].bitcast(U32).indirect(entries))
            product(2, half, xw_last[:], xs[4:P, columns(half)])

        def empty_banks(copy, half, first):
            for t in (first, first + 1):
                copy(y[half][:, t, :], acc[half][t][:])
            nc.sync.dma_start(out_rows[:, first : first + 2, columns(half)], y[half][:, first : first + 2, :])

        def hand_on(half):
            quantize(y_codes[half][:], y_scales[:, columns(half)], y_bf[half][:].rearrange("p c t -> p (c t)"))
            nc.sync.dma_start(out_words[:, columns(half)], y_codes[half][:].bitcast(I32))

        empty_banks(nc.scalar.copy, 0, 0)
        empty_banks(nc.vector.tensor_copy, 0, 2)
        regroup(nc.vector.tensor_copy, y_bf[0][:], y[0][:])
        hand_on(0)
        empty_banks(nc.scalar.copy, 1, 0)
        empty_banks(nc.scalar.copy, 1, 2)
        regroup(nc.scalar.copy, y_bf[1][:, :LAST_RESULT_ON_SCALAR, :], y[1][:, :, :LAST_RESULT_ON_SCALAR])
        regroup(nc.vector.tensor_copy, y_bf[1][:, LAST_RESULT_ON_SCALAR:, :], y[1][:, :, LAST_RESULT_ON_SCALAR:])
        hand_on(1)

        for q in range(QUADRANTS):
            queue = nc.sync if q % 2 == 0 else nc.scalar
            queue.dma_start(
                out_2[0, 4 * q : 4 * q + 4, :].bitcast(I32),
                y_scales[32 * q : 32 * q + 4, :].bitcast(I32),
            )
